import numpy as np
CORES = [6,14,22,30,38,46,54,62,70,78,86,94,102,110,118,126,134,142,150,158,166,174,182,190,198,206,214,222,230,238,246,254]
N = 32
ROUNDS = 6
def setup_inputs(rng):
    return {"x": rng.standard_normal((N, ROUNDS, 128, 16), dtype=np.float32)}
def reference(x):
    g = np.concatenate(list(x), axis=2)
    return {"y": np.broadcast_to(g, (N,) + g.shape)}

@@ -1,0 +1,39 @@
+from concourse.bass import RemoteDMATransfer, DstId
+
+SCRATCH = {
+    "land": ("sbuf", [128, 2, 512], "float32"),
+}
+SEMAPHORES = ["dma", "a0", "a1"]
+
+
+def rank_program(g, core, T, topo):
+    rank = T.rank_of(core)
+    if rank is None:
+        return
+    rounds = T.x.shape[0]
+    w = T.x.shape[2]
+    arr = [T.sem.a0, T.sem.a1]
+    cnt = [0, 0]
+    ndma = 0
+    others = [c for c in T.cores if c != core]
+    halves = [others[:16], others[16:]]
+    for k in range(rounds):
+        s = k % 2
+        own = T.land[:, s, rank * w:(rank + 1) * w]
+        g.dma_start(own, T.x[k]).then_inc(T.sem.dma, 16)
+        ndma += 16
+        g.wait_ge(T.sem.dma, ndma)
+        trs = []
+        for h, m in zip(halves, (0x0F, 0xF0)):
+            ids = []
+            for d in h:
+                rid, pid = topo.addr(d, core)
+                ids.append(DstId(rid=rid, pnc=pid))
+            trs.append(RemoteDMATransfer(dst_ids=ids, dma_engine_mask=m, remote_sem=arr[s],
+                                         srcs=[own], dsts=[own for d in h]))
+        g.remote_dma_fused(trs, local_sem=arr[s])
+        cnt[s] += 31 * 4 + 8
+        g.wait_ge(arr[s], cnt[s])
+        g.dma_start(T.y[k], T.land[:, s, :]).then_inc(T.sem.dma, 16)
+        ndma += 16
+    g.wait_ge(T.sem.dma, ndma)

@@ -2,38 +2,110 @@ from concourse.bass import RemoteDMATransfer, DstId
 
 SCRATCH = {
     "land": ("sbuf", [128, 2, 512], "float32"),
+    "stq": ("sbuf", [128, 2, 16], "float32"),
+    "xq": ("sbuf", [128, 16], "float32"),
 }
-SEMAPHORES = ["dma", "a0", "a1"]
+SEMAPHORES = ["dma", "A", "B"]
+
+OFF = 0xFF
 
 
 def rank_program(g, core, T, topo):
     rank = T.rank_of(core)
     if rank is None:
         return
-    rounds = T.x.shape[0]
     w = T.x.shape[2]
-    arr = [T.sem.a0, T.sem.a1]
-    cnt = [0, 0]
-    ndma = 0
-    others = [c for c in T.cores if c != core]
-    halves = [others[:16], others[16:]]
-    for k in range(rounds):
-        s = k % 2
-        own = T.land[:, s, rank * w:(rank + 1) * w]
-        g.dma_start(own, T.x[k]).then_inc(T.sem.dma, 16)
-        ndma += 16
-        g.wait_ge(T.sem.dma, ndma)
-        trs = []
-        for h, m in zip(halves, (0x0F, 0xF0)):
-            ids = []
-            for d in h:
-                rid, pid = topo.addr(d, core)
-                ids.append(DstId(rid=rid, pnc=pid))
-            trs.append(RemoteDMATransfer(dst_ids=ids, dma_engine_mask=m, remote_sem=arr[s],
-                                         srcs=[own], dsts=[own for d in h]))
-        g.remote_dma_fused(trs, local_sem=arr[s])
-        cnt[s] += 31 * 4 + 8
-        g.wait_ge(arr[s], cnt[s])
-        g.dma_start(T.y[k], T.land[:, s, :]).then_inc(T.sem.dma, 16)
-        ndma += 16
-    g.wait_ge(T.sem.dma, ndma)
+    width = T.y.shape[2]
+    turns = T.x.shape[0] // 2
+    par = rank % 2
+    sd, sl = par, 1 - par
+    rd = [2 * j + par for j in range(turns)]
+    rl = [2 * j + 1 - par for j in range(turns)]
+    mrank = rank ^ 1
+    mate = T.cores[mrank]
+    peers = [T.cores[i] for i in range(len(T.cores)) if i % 2 == par and i != rank]
+    A, B, D = T.sem.A, T.sem.B, T.sem.dma
+    cnt = {"A": 0, "B": 0, "D": 0}
+
+    def dst(c):
+        rid, pid = topo.addr(c, core)
+        return DstId(rid=rid, pnc=pid)
+
+    def local(out, in_):
+        g.dma_start(out, in_).then_inc(D, 16)
+        cnt["D"] += 16
+
+    def wait_local():
+        g.wait_ge(D, cnt["D"])
+
+    def to_mate(out_ap, in_ap, rsem, lsem):
+        rid, pid = topo.addr(mate, core)
+        g.remote_dma(out_ap, in_ap, rsem, lsem, pid, rid, OFF)
+
+    def cols(s, r):
+        return T.land[:, s, r * w:(r + 1) * w]
+
+    def f_ranges(skip):
+        out = []
+        if skip > 0:
+            out.append((0, skip * w))
+        if (skip + 1) * w < width:
+            out.append(((skip + 1) * w, width))
+        return out
+
+    pair_lo = (rank // 2) * 2 * w
+    pair = T.land[:, sd, pair_lo:pair_lo + 2 * w]
+    nf_out = len(f_ranges(mrank))
+    nf_in = len(f_ranges(rank))
+
+    local(cols(sl, rank), T.x[rl[0]])
+    local(cols(sd, rank), T.x[rd[0]])
+    local(T.xq[:], T.x[rl[1]])
+    wait_local()
+    to_mate(cols(sl, rank), cols(sl, rank), B, B)
+    cnt["B"] += 8 + 8
+    g.wait_ge(B, cnt["B"])
+
+    for j in range(turns):
+        last = j == turns - 1
+        g.remote_dma_fused(
+            [RemoteDMATransfer(dst_ids=[dst(c) for c in peers], dma_engine_mask=OFF, remote_sem=A,
+                               srcs=[pair], dsts=[pair for c in peers])],
+            local_sem=A)
+        cnt["A"] += 8 + 8 * len(peers)
+        if not last:
+            to_mate(T.stq[:, j, :], T.xq[:], A, A)
+            cnt["A"] += 8 + 8
+        else:
+            rid, pid = topo.addr(mate, core)
+            g.remote_sem_update(A, A, pid, rid, 0x01)
+            cnt["A"] += 1 + 1
+        g.wait_ge(A, cnt["A"])
+
+        for lo, hi in f_ranges(mrank):
+            to_mate(T.land[:, sd, lo:hi], T.land[:, sd, lo:hi], B, B if last else A)
+        local(T.y[rd[j]], T.land[:, sd, :])
+        if not last:
+            cnt["A"] += 8 * nf_out
+            g.wait_ge(A, cnt["A"])
+            wait_local()
+            targets = peers + [mate]
+            for i in range(0, len(targets), 8):
+                g.remote_dma_fused(
+                    [RemoteDMATransfer(dst_ids=[dst(c)], dma_engine_mask=1 << e, remote_sem=B)
+                     for e, c in enumerate(targets[i:i + 8])],
+                    local_sem=B)
+            cnt["B"] += len(targets) + len(targets)
+            local(cols(sd, rank), T.x[rd[j + 1]])
+            local(cols(sd, mrank), T.stq[:, j, :])
+            if j + 2 < turns:
+                local(T.xq[:], T.x[rl[j + 2]])
+        else:
+            cnt["B"] += 8 * nf_out
+        cnt["B"] += 8 * nf_in
+        g.wait_ge(B, cnt["B"])
+        local(T.y[rl[j]], T.land[:, sl, :])
+        wait_local()
+        if not last:
+            local(cols(sl, rank), T.x[rl[j + 1]])
+            wait_local()

@@ -2,7 +2,8 @@ from concourse.bass import RemoteDMATransfer, DstId
 
 SCRATCH = {
     "land": ("sbuf", [128, 2, 512], "float32"),
-    "stq": ("sbuf", [128, 2, 16], "float32"),
+    "fp": ("sbuf", [128, 32], "float32"),
+    "stq": ("sbuf", [128, 16], "float32"),
     "xq": ("sbuf", [128, 16], "float32"),
 }
 SEMAPHORES = ["dma", "A", "B"]
@@ -14,6 +15,7 @@ def rank_program(g, core, T, topo):
     rank = T.rank_of(core)
     if rank is None:
         return
+    n = len(T.cores)
     w = T.x.shape[2]
     width = T.y.shape[2]
     turns = T.x.shape[0] // 2
@@ -21,9 +23,12 @@ def rank_program(g, core, T, topo):
     sd, sl = par, 1 - par
     rd = [2 * j + par for j in range(turns)]
     rl = [2 * j + 1 - par for j in range(turns)]
+    half = n // 2
     mrank = rank ^ 1
     mate = T.cores[mrank]
-    peers = [T.cores[i] for i in range(len(T.cores)) if i % 2 == par and i != rank]
+    cpart = T.cores[rank ^ half]
+    diag = T.cores[rank ^ half ^ 1]
+    peers = [T.cores[i] for i in range(n) if i % 2 == par and i // half == rank // half and i != rank]
     A, B, D = T.sem.A, T.sem.B, T.sem.dma
     cnt = {"A": 0, "B": 0, "D": 0}
 
@@ -42,6 +47,17 @@ def rank_program(g, core, T, topo):
         rid, pid = topo.addr(mate, core)
         g.remote_dma(out_ap, in_ap, rsem, lsem, pid, rid, OFF)
 
+    def copy_to(cores, mask, sem, src, out):
+        return RemoteDMATransfer(dst_ids=[dst(c) for c in cores], dma_engine_mask=mask, remote_sem=sem,
+                                 srcs=[src], dsts=[out for c in cores])
+
+    def signal(c, mask, sem):
+        return RemoteDMATransfer(dst_ids=[dst(c)], dma_engine_mask=mask, remote_sem=sem)
+
+    def signal_to(c, sem):
+        rid, pid = topo.addr(c, core)
+        g.remote_sem_update(sem, sem, pid, rid, 0x01)
+
     def cols(s, r):
         return T.land[:, s, r * w:(r + 1) * w]
 
@@ -53,8 +69,10 @@ def rank_program(g, core, T, topo):
             out.append(((skip + 1) * w, width))
         return out
 
-    pair_lo = (rank // 2) * 2 * w
-    pair = T.land[:, sd, pair_lo:pair_lo + 2 * w]
+    home_lo = (rank // 2) * 2 * w
+    away_lo = (home_lo + width // 2) % width
+    home = T.land[:, sd, home_lo:home_lo + 2 * w]
+    away = T.land[:, sd, away_lo:away_lo + 2 * w]
     nf_out = len(f_ranges(mrank))
     nf_in = len(f_ranges(rank))
 
@@ -62,24 +80,25 @@ def rank_program(g, core, T, topo):
     local(cols(sd, rank), T.x[rd[0]])
     local(T.xq[:], T.x[rl[1]])
     wait_local()
-    to_mate(cols(sl, rank), cols(sl, rank), B, B)
-    cnt["B"] += 8 + 8
+    g.remote_dma_fused(
+        [copy_to([mate, diag], 0x0F, B, cols(sl, rank), cols(sl, rank)),
+         copy_to([cpart], 0xF0, B, cols(sd, rank), cols(sd, rank))],
+        local_sem=B)
+    cnt["B"] += 8 + 3 * 4
     g.wait_ge(B, cnt["B"])
 
     for j in range(turns):
         last = j == turns - 1
         g.remote_dma_fused(
-            [RemoteDMATransfer(dst_ids=[dst(c) for c in peers], dma_engine_mask=OFF, remote_sem=A,
-                               srcs=[pair], dsts=[pair for c in peers])],
+            [copy_to(peers, 0x0F, A, home, home),
+             copy_to(peers, 0xF0, A, away, away)],
             local_sem=A)
         cnt["A"] += 8 + 8 * len(peers)
+        signal_to(mate if last else cpart, A)
+        cnt["A"] += 1 + 1
         if not last:
-            to_mate(T.stq[:, j, :], T.xq[:], A, A)
+            to_mate(T.stq[:], T.xq[:], A, A)
             cnt["A"] += 8 + 8
-        else:
-            rid, pid = topo.addr(mate, core)
-            g.remote_sem_update(A, A, pid, rid, 0x01)
-            cnt["A"] += 1 + 1
         g.wait_ge(A, cnt["A"])
 
         for lo, hi in f_ranges(mrank):
@@ -89,22 +108,25 @@ def rank_program(g, core, T, topo):
             cnt["A"] += 8 * nf_out
             g.wait_ge(A, cnt["A"])
             wait_local()
-            targets = peers + [mate]
-            for i in range(0, len(targets), 8):
-                g.remote_dma_fused(
-                    [RemoteDMATransfer(dst_ids=[dst(c)], dma_engine_mask=1 << e, remote_sem=B)
-                     for e, c in enumerate(targets[i:i + 8])],
-                    local_sem=B)
-            cnt["B"] += len(targets) + len(targets)
+            g.remote_dma_fused([signal(c, 1 << e, B) for e, c in enumerate(peers)], local_sem=B)
+            cnt["B"] += len(peers) + len(peers)
             local(cols(sd, rank), T.x[rd[j + 1]])
-            local(cols(sd, mrank), T.stq[:, j, :])
+            local(cols(sd, mrank), T.stq[:])
             if j + 2 < turns:
                 local(T.xq[:], T.x[rl[j + 2]])
+            wait_local()
+            rid, pid = topo.addr(cpart, core)
+            g.remote_dma(T.fp[:], home, B, B, pid, rid, OFF)
+            cnt["B"] += 8 + 8
+            signal_to(mate, B)
+            cnt["B"] += 1 + 1
         else:
             cnt["B"] += 8 * nf_out
         cnt["B"] += 8 * nf_in
         g.wait_ge(B, cnt["B"])
         local(T.y[rl[j]], T.land[:, sl, :])
+        if not last:
+            local(away, T.fp[:])
         wait_local()
         if not last:
             local(cols(sl, rank), T.x[rl[j + 1]])

@@ -124,10 +124,10 @@ def rank_program(g, core, T, topo):
             cnt["B"] += 8 * nf_out
         cnt["B"] += 8 * nf_in
         g.wait_ge(B, cnt["B"])
+        wait_local()
         local(T.y[rl[j]], T.land[:, sl, :])
         if not last:
             local(away, T.fp[:])
         wait_local()
         if not last:
             local(cols(sl, rank), T.x[rl[j + 1]])
-            wait_local()

from concourse.bass import RemoteDMATransfer, DstId

SCRATCH = {
    "land": ("sbuf", [128, 2, 512], "float32"),
    "fp": ("sbuf", [128, 32], "float32"),
    "stq": ("sbuf", [128, 16], "float32"),
    "xq": ("sbuf", [128, 16], "float32"),
}
SEMAPHORES = ["dma", "A", "B"]

OFF = 0xFF


def rank_program(g, core, T, topo):
    rank = T.rank_of(core)
    if rank is None:
        return
    n = len(T.cores)
    w = T.x.shape[2]
    width = T.y.shape[2]
    turns = T.x.shape[0] // 2
    par = rank % 2
    sd, sl = par, 1 - par
    rd = [2 * j + par for j in range(turns)]
    rl = [2 * j + 1 - par for j in range(turns)]
    half = n // 2
    mrank = rank ^ 1
    mate = T.cores[mrank]
    cpart = T.cores[rank ^ half]
    diag = T.cores[rank ^ half ^ 1]
    peers = [T.cores[i] for i in range(n) if i % 2 == par and i // half == rank // half and i != rank]
    A, B, D = T.sem.A, T.sem.B, T.sem.dma
    cnt = {"A": 0, "B": 0, "D": 0}

    def dst(c):
        rid, pid = topo.addr(c, core)
        return DstId(rid=rid, pnc=pid)

    def local(out, in_):
        g.dma_start(out, in_).then_inc(D, 16)
        cnt["D"] += 16

    def wait_local():
        g.wait_ge(D, cnt["D"])

    def to_mate(out_ap, in_ap, rsem, lsem):
        rid, pid = topo.addr(mate, core)
        g.remote_dma(out_ap, in_ap, rsem, lsem, pid, rid, OFF)

    def copy_to(cores, mask, sem, src, out):
        return RemoteDMATransfer(dst_ids=[dst(c) for c in cores], dma_engine_mask=mask, remote_sem=sem,
                                 srcs=[src], dsts=[out for c in cores])

    def signal(c, mask, sem):
        return RemoteDMATransfer(dst_ids=[dst(c)], dma_engine_mask=mask, remote_sem=sem)

    def signal_to(c, sem):
        rid, pid = topo.addr(c, core)
        g.remote_sem_update(sem, sem, pid, rid, 0x01)

    def cols(s, r):
        return T.land[:, s, r * w:(r + 1) * w]

    def f_ranges(skip):
        out = []
        if skip > 0:
            out.append((0, skip * w))
        if (skip + 1) * w < width:
            out.append(((skip + 1) * w, width))
        return out

    home_lo = (rank // 2) * 2 * w
    away_lo = (home_lo + width // 2) % width
    home = T.land[:, sd, home_lo:home_lo + 2 * w]
    away = T.land[:, sd, away_lo:away_lo + 2 * w]
    nf_out = len(f_ranges(mrank))
    nf_in = len(f_ranges(rank))

    local(cols(sl, rank), T.x[rl[0]])
    local(cols(sd, rank), T.x[rd[0]])
    local(T.xq[:], T.x[rl[1]])
    wait_local()
    g.remote_dma_fused(
        [copy_to([mate, diag], 0x0F, B, cols(sl, rank), cols(sl, rank)),
         copy_to([cpart], 0xF0, B, cols(sd, rank), cols(sd, rank))],
        local_sem=B)
    cnt["B"] += 8 + 3 * 4
    g.wait_ge(B, cnt["B"])

    for j in range(turns):
        last = j == turns - 1
        g.remote_dma_fused(
            [copy_to(peers, 0x0F, A, home, home),
             copy_to(peers, 0xF0, A, away, away)],
            local_sem=A)
        cnt["A"] += 8 + 8 * len(peers)
        signal_to(mate if last else cpart, A)
        cnt["A"] += 1 + 1
        if not last:
            to_mate(T.stq[:], T.xq[:], A, A)
            cnt["A"] += 8 + 8
        g.wait_ge(A, cnt["A"])

        for lo, hi in f_ranges(mrank):
            to_mate(T.land[:, sd, lo:hi], T.land[:, sd, lo:hi], B, B if last else A)
        local(T.y[rd[j]], T.land[:, sd, :])
        if not last:
            cnt["A"] += 8 * nf_out
            g.wait_ge(A, cnt["A"])
            wait_local()
            g.remote_dma_fused([signal(c, 1 << e, B) for e, c in enumerate(peers)], local_sem=B)
            cnt["B"] += len(peers) + len(peers)
            local(cols(sd, rank), T.x[rd[j + 1]])
            local(cols(sd, mrank), T.stq[:])
            if j + 2 < turns:
                local(T.xq[:], T.x[rl[j + 2]])
            wait_local()
            rid, pid = topo.addr(cpart, core)
            g.remote_dma(T.fp[:], home, B, B, pid, rid, OFF)
            cnt["B"] += 8 + 8
            signal_to(mate, B)
            cnt["B"] += 1 + 1
        else:
            cnt["B"] += 8 * nf_out
        cnt["B"] += 8 * nf_in
        g.wait_ge(B, cnt["B"])
        wait_local()
        local(T.y[rl[j]], T.land[:, sl, :])
        if not last:
            local(away, T.fp[:])
        wait_local()
        if not last:
            local(cols(sl, rank), T.x[rl[j + 1]])
